import numpy as np
import ml_dtypes

BF16 = ml_dtypes.bfloat16


def bf(x):
    return np.asarray(x, np.float32).astype(BF16)


def f32(x):
    return np.asarray(x, np.float32)


def f64(x):
    return np.asarray(x).astype(np.float64)


def striped(idx):
    return np.tile(idx.reshape(-1, 16).T, (8, 1))


def rows(idx, k):
    return np.tile(idx, (k, 1))


def look(tab, idx):
    return np.take_along_axis(f64(tab), rows(idx, len(tab)), axis=1)


K, S, D, V, N = 128, 256, 2, 128, 256


def setup_inputs():
    return {"tab": f32(np.random.standard_normal((K, S))), "th": f32(np.random.standard_normal((K, V))), "offs": striped(np.random.permutation(S)[:N])}


def reference(tab, th, offs):
    idx = offs[:16].T.reshape(-1)
    x = sum((look(tab, idx[d * V:(d + 1) * V]) >= f64(th)) * 1.0 for d in range(D)) / D
    return x

import concourse.mybir as mybir

F32, U16 = mybir.dt.float32, mybir.dt.uint16
IS_GE, MULT, ADD = mybir.AluOpType.is_ge, mybir.AluOpType.mult, mybir.AluOpType.add

ROWS = 128
COLUMNS = 256
V = 128
D = 2
LIST_COLUMNS = D * V // 16


def tile_lookup_vote_ge_out_kernel(tc, tab, th, offs, out):
    nc = tc.nc
    with tc.tile_pool(name="held", bufs=1) as held:
        offsets = held.tile([ROWS, LIST_COLUMNS], U16, name="offsets")
        table = held.tile([ROWS, COLUMNS], F32, name="table")
        thresholds = held.tile([ROWS, V], F32, name="thresholds")
        nc.sync.dma_start(offsets[:], offs)
        nc.scalar.dma_start(table[:], tab)
        nc.sync.dma_start(thresholds[:], th)

        votes = [held.tile([ROWS, V], F32, name=f"votes{d}") for d in range(D)]
        for d in range(D):
            piece = offsets[:, d * V // 16 : (d + 1) * V // 16]
            nc.vector.tensor_tensor(votes[d][:], table[:].indirect(piece), thresholds[:], IS_GE)

        halved = held.tile([ROWS, V], F32, name="halved")
        share = held.tile([ROWS, V], F32, name="share")
        nc.vector.tensor_scalar(halved[:], votes[0][:], 1.0 / D, None, MULT)
        nc.vector.scalar_tensor_tensor(share[:], votes[1][:], 1.0 / D, halved[:], MULT, ADD)
        nc.sync.dma_start(out, share[:])
